import numpy as np
import ml_dtypes


def mxq(x, axis, fmt="e4m3"):
    dtype, down = {"e4m3": (ml_dtypes.float8_e4m3fn, 7), "e5m2": (ml_dtypes.float8_e5m2, 14)}[fmt]
    v = np.moveaxis(np.asarray(x, np.float32).astype(ml_dtypes.bfloat16).astype(np.float64), axis, -1)
    blocks = v.reshape(v.shape[:-1] + (-1, 32))
    amax = np.abs(blocks).max(-1, keepdims=True)
    byte = np.maximum(np.where(amax > 0, np.frexp(amax)[1] - 1 + 127, 0) - down, 1)
    scale = np.exp2(byte - 127.0)
    codes = (blocks / scale).astype(np.float32).astype(dtype).astype(np.float64)
    return np.moveaxis((codes * scale).reshape(v.shape), -1, axis)


WIDE = False


def mx_kscale(k):
    if not WIDE:
        return np.ones(k)
    levels = np.array([10, -10, 5, -5, 0])
    if k % 512:
        return np.exp2(np.random.permutation(np.resize(levels, k // 32))).repeat(32)
    a = np.empty((k // 512, 16))
    for p in range(k // 512):
        a[p, :8] = np.random.permutation(np.resize(levels, 8))
        for g in range(8):
            far = levels[np.abs(levels - a[p, g]) >= 10]
            a[p, g + 8] = far[np.random.randint(len(far))]
    return np.exp2(a.ravel()).repeat(32)


def f64(x):
    return np.asarray(x).astype(np.float64)


E2M1 = np.array([0.0, 0.5, 1.0, 1.5, 2.0, 3.0, 4.0, 6.0, -0.0, -0.5, -1.0, -1.5, -2.0, -3.0, -4.0, -6.0])


def pack_weight(w, fmt):
    k, n = w.shape
    w = f64(np.asarray(w, np.float32).astype(ml_dtypes.bfloat16)).reshape(k // 32, 32, n)
    amax = np.abs(w).max(1)
    if fmt == "e4m3":
        byte = np.frexp(amax)[1] - 1 + 127 - 7
    else:
        mant, ex = np.frexp(amax / 6.0)
        byte = np.where(mant > 0.5, ex, ex - 1) + 127
    byte = np.clip(np.where(amax > 0, byte, 1), 1, 254)
    scaled = (w * np.exp2(127.0 - byte)[:, None, :]).reshape(k, n).astype(np.float32)
    by_word = np.ascontiguousarray(scaled.reshape(k // 512, 128, 4, n).transpose(0, 1, 3, 2))
    if fmt == "e4m3":
        words = by_word.astype(ml_dtypes.float8_e4m3fn).view(np.uint8)
    else:
        c = by_word.astype(ml_dtypes.float4_e2m1fn).view(np.uint8) & 0xF
        words = (c[..., 0::2] | (c[..., 1::2] << 4)).reshape(k // 512, 128, 2 * n)
    return np.ascontiguousarray(words), np.ascontiguousarray(byte.astype(np.uint8).reshape(k // 512, 16, n))


def unpack_weight(words, scales, fmt):
    g, _, n = scales.shape
    words = np.ascontiguousarray(words).reshape(g, 128, n, -1)
    if fmt == "e4m3":
        vals = words.view(ml_dtypes.float8_e4m3fn).astype(np.float64)
    else:
        nib = np.empty((g, 128, n, 4), np.uint8)
        nib[..., 0::2] = words & 0xF
        nib[..., 1::2] = words >> 4
        vals = E2M1[nib]
    vals = vals * np.repeat(np.exp2(scales.astype(np.float64) - 127.0), 8, axis=1)[..., None]
    return vals.transpose(0, 1, 3, 2).reshape(g * 512, n)


def planes(y):
    n, m = y.shape
    v = y.astype(np.float32).astype(ml_dtypes.bfloat16).astype(np.float64).reshape(n // 32, 32, m)
    top = np.abs(v).max(1)
    byte = np.clip(np.where(top > 0, np.frexp(top)[1] - 1 + 127 - 7, 1), 1, 254)
    codes = (v * np.exp2(127.0 - byte)[:, None, :]).reshape(n, m).astype(np.float32).astype(ml_dtypes.float8_e4m3fn).view(np.uint8)
    words = codes.reshape(n // 512, 128, 4, m).transpose(0, 1, 3, 2)
    return np.ascontiguousarray(words), np.ascontiguousarray(byte.astype(np.uint8).reshape(n // 512, 16, m))


def silu(v):
    return v / (1.0 + np.exp(-np.maximum(v, -700.0)))


K, M, T = 1024, 1536, 512


def setup_inputs():
    n = np.random.standard_normal
    s = mx_kscale(K)[:, None]
    p_w4 = pack_weight(n((K, M)) / np.sqrt(K) / s, "e2m1")
    p_w8 = pack_weight(n((K, M)) / np.sqrt(K) / s, "e4m3")
    return {
        "x": (n((K, T)) * s).astype(np.float32),
        "w4_words": p_w4[0],
        "w4_scales": p_w4[1],
        "w8_words": p_w8[0],
        "w8_scales": p_w8[1],
        "b": (0.3 * n(1536)).astype(np.float32),
    }


def reference(x, w4_words, w4_scales, w8_words, w8_scales, b):
    xa_, xb_ = mxq(np.maximum(f64(x), 0.0), 0, "e4m3"), mxq(np.maximum(-f64(x), 0.0), 0, "e4m3")
    w4_ = unpack_weight(w4_words, w4_scales, "e2m1")
    w8_ = unpack_weight(w8_words, w8_scales, "e4m3")
    y = w4_.T @ xa_ + w8_.T @ xb_
    out_0 = silu(y + f64(b)[:, None])
    return (out_0,) + planes(out_0)

@@ -1,0 +1,281 @@
+from contextlib import ExitStack
+
+import concourse.mybir as mybir
+
+K, M, T = 1024, 1536, 512
+FLOPS = 2 * 2 * K * M * T
+
+F32 = mybir.dt.float32
+BF16 = mybir.dt.bfloat16
+I32 = mybir.dt.int32
+U32 = mybir.dt.uint32
+U8 = mybir.dt.uint8
+FP8X4 = mybir.dt.float8_e4m3fn_x4
+FP4X4 = mybir.dt.float4_e2m1fn_x4
+ALU = mybir.AluOpType
+ACT = mybir.ActivationFunctionType
+
+P = 128
+PACK = 4
+SPAN = P * PACK
+PASSES = K // SPAN
+GROUPS = M // SPAN
+HALF = T // 2
+QUADS = 4
+W8_ROW = 4
+
+
+def tile_mix_feat_fm_crelupl_silu_kernel(
+    tc, x, w4_words, w4_scales, w8_words, w8_scales, b, out_0, out_1, out_2
+):
+    nc = tc.nc
+    with ExitStack() as ctx:
+        sb = ctx.enter_context(tc.tile_pool(name="sb", bufs=1))
+        ps = ctx.enter_context(tc.psum_pool(name="ps", bufs=1))
+        ctx.enter_context(tc.manual_schedule())
+
+        def tile(name, shape, dtype):
+            return sb.tile(shape, dtype, name=name, align_bytes=64)
+
+        x_raw = {(a, h): tile("x_raw%d%d" % (a, h), [P, PACK, HALF], F32) for a in range(PASSES) for h in range(2)}
+        feat = {(s, a): tile("feat%s%d" % (s, a), [P, T, PACK], BF16) for s in "ab" for a in range(PASSES)}
+        x_codes = {(s, a): tile("x_codes%s%d" % (s, a), [P, T], U32) for s in "ab" for a in range(PASSES)}
+        x_scales = {(s, a): tile("x_scales%s%d" % (s, a), [P, T], U8) for s in "ab" for a in range(PASSES)}
+        w4_raw = {a: tile("w4_raw%d" % a, [P, 2 * M], U8) for a in range(PASSES)}
+        w8_raw = {(a, g): tile("w8_raw%d%d" % (a, g), [P, SPAN], I32) for a in range(PASSES) for g in range(GROUPS)}
+        ws_raw = tile("ws_raw", [P, PASSES, M], U8)
+        w4 = {(a, g): tile("w4_%d%d" % (a, g), [P, PACK, 2 * P], U8) for a in range(PASSES) for g in range(GROUPS)}
+        w8 = {(a, g): tile("w8_%d%d" % (a, g), [P, PACK, P], I32) for a in range(PASSES) for g in range(GROUPS)}
+        ws = {(a, g): tile("ws_%d%d" % (a, g), [P, PACK, P], U8) for a in range(PASSES) for g in range(GROUPS)}
+        bias = tile("bias", [P, GROUPS, PACK], F32)
+        y = {g: tile("y%d" % g, [P, PACK, T], F32) for g in range(GROUPS)}
+        y_bf = {g: tile("y_bf%d" % g, [P, T, PACK], BF16) for g in range(GROUPS)}
+        y_codes = {g: tile("y_codes%d" % g, [P, T], U32) for g in range(GROUPS)}
+        y_scales = tile("y_scales", [P, GROUPS, T], U8)
+        warm = tile("warm", [P, 16], F32)
+        acc = {}
+
+        def load_x(a, h):
+            rows = x[a * SPAN : (a + 1) * SPAN, :].rearrange("(p j) t -> p j t", j=PACK)
+            nc.sync.dma_start(out=x_raw[a, h][:], in_=rows[:, :, h * HALF : (h + 1) * HALF])
+
+        def load_w4(a, g0, g1):
+            cols = slice(2 * SPAN * g0, 2 * SPAN * g1)
+            nc.sync.dma_start(out=w4_raw[a][:, cols].bitcast(I32), in_=w4_words[a][:, cols].bitcast(I32))
+
+        def load_w8(a, g):
+            src = w8_words[a].rearrange("p n i -> p (n i)")
+            nc.sync.dma_start(out=w8_raw[a, g][:], in_=src[:, PACK * SPAN * g : PACK * SPAN * (g + 1)].bitcast(I32))
+
+        def load_scales(queue, src, row, quads):
+            for q in quads:
+                queue.dma_start(
+                    out=ws_raw[32 * q + row : 32 * q + row + 4, :, :].bitcast(I32),
+                    in_=src[:, 4 * q : 4 * q + 4, :].rearrange("a q n -> q a n").bitcast(I32),
+                )
+
+        def feat_views(s, a, h):
+            dst = feat[s, a][:, h * HALF : (h + 1) * HALF, :].rearrange("p (c i) j -> p c j i", i=4)
+            src = x_raw[a, h][:].rearrange("p j (c i) -> p c j i", i=4)
+            return dst, src
+
+        def feat_vector(s, a, h):
+            dst, src = feat_views(s, a, h)
+            sign = 1.0 if s == "a" else -1.0
+            nc.vector.tensor_scalar(out=dst, in0=src, scalar1=sign, scalar2=0.0, op0=ALU.mult, op1=ALU.max)
+
+        def feat_scalar(s, a, h):
+            dst, src = feat_views(s, a, h)
+            sign = 1.0 if s == "a" else -1.0
+            nc.scalar.activation(out=dst, in_=src, func=ACT.Relu, scale=sign)
+
+        def quant_x(s, a, h):
+            cols = slice(h * HALF, (h + 1) * HALF)
+            nc.vector.quantize_mx(
+                out=x_codes[s, a][:, cols].bitcast(FP8X4),
+                scales=x_scales[s, a][:, cols],
+                in_=feat[s, a][:, cols, :].rearrange("p t j -> p (t j)"),
+            )
+
+        def deal_w4(a, g):
+            src = w4_raw[a][:, 2 * SPAN * g : 2 * SPAN * (g + 1)]
+            nc.vector.tensor_copy(
+                out=w4[a, g][:].rearrange("p r (m e) -> p r m e", e=2),
+                in_=src.rearrange("p (m r e) -> p r m e", r=PACK, e=2),
+            )
+
+        def deal_w8(a, g):
+            nc.vector.tensor_copy(
+                out=w8[a, g][:].rearrange("p r m -> p m r"),
+                in_=w8_raw[a, g][:].rearrange("p (m r) -> p m r", r=PACK),
+            )
+
+        def deal_scales(a, g):
+            src = ws_raw[:, a, SPAN * g : SPAN * (g + 1)]
+            nc.vector.tensor_copy(out=ws[a, g][:], in_=src.rearrange("p (m r) -> p r m", r=PACK))
+
+        def mm4(a, g, r, c0=0, n=T):
+            cols = slice(c0, c0 + n)
+            if a == 0:
+                bank = len(acc) % 8
+                acc[g, r, c0] = ps.tile([P, T], F32, name="acc%d" % len(acc), tag="bank%d" % bank)
+            nc.tensor.matmul_mx(
+                out=acc[g, r, c0][:, 0:n],
+                lhsT=w4[a, g][:, r, :].bitcast(FP4X4),
+                lhsT_scale=ws[a, g][:, r, :],
+                rhs=x_codes["a", a][:, cols].bitcast(FP8X4),
+                rhs_scale=x_scales["a", a][:, cols],
+                start=(a == 0),
+                stop=False,
+            )
+
+        def mm8(a, g, r, c0=0, n=T):
+            cols = slice(c0, c0 + n)
+            nc.tensor.matmul_mx(
+                out=acc[g, r, c0][:, 0:n],
+                lhsT=w8[a, g][:, r, :].bitcast(FP8X4),
+                lhsT_scale=ws[a, g][W8_ROW:P, r, :],
+                rhs=x_codes["b", a][:, cols].bitcast(FP8X4),
+                rhs_scale=x_scales["b", a][:, cols],
+                start=False,
+                stop=(a == PASSES - 1),
+            )
+
+        def silu(g, r, c0=0, n=T):
+            nc.scalar.activation(
+                out=y[g][:, r, c0 : c0 + n], in_=acc[g, r, c0][:, 0:n], func=ACT.Silu, bias=bias[:, g, r : r + 1]
+            )
+
+        def store_y(queue, g, r):
+            rows = out_0[g * SPAN : (g + 1) * SPAN, :].rearrange("(p r) t -> p r t", r=PACK)
+            queue.dma_start(out=rows[:, r, :], in_=y[g][:, r, :])
+
+        def silu_store(g, r):
+            silu(g, r)
+            store_y(nc.sync, g, r)
+
+        def round_y(g, c0, n):
+            cols = slice(c0, c0 + n)
+            nc.vector.tensor_copy(
+                out=y_bf[g][:, cols, :].rearrange("p (c i) r -> p c r i", i=4),
+                in_=y[g][:, :, cols].rearrange("p r (c i) -> p c r i", i=4),
+            )
+
+        def quant_y(g, c0, n):
+            cols = slice(c0, c0 + n)
+            nc.vector.quantize_mx(
+                out=y_codes[g][:, cols].bitcast(FP8X4),
+                scales=y_scales[:, g, cols],
+                in_=y_bf[g][:, cols, :].rearrange("p t r -> p (t r)"),
+            )
+
+        def store_codes(g, c0, n):
+            cols = slice(c0, c0 + n)
+            nc.sync.dma_start(
+                out=out_1[g].rearrange("p t i -> p (t i)").bitcast(I32)[:, cols], in_=y_codes[g][:, cols].bitcast(I32)
+            )
+
+        def planes(g):
+            round_y(g, 0, HALF)
+            round_y(g, HALF, HALF)
+            quant_y(g, 0, HALF)
+            quant_y(g, HALF, HALF)
+            store_codes(g, 0, T)
+
+        nc.vector.memset(ws_raw[:].rearrange("p a n -> p (a n)").bitcast(I32), 0)
+        nc.vector.memset(warm[:], 0.0)
+        nc.scalar.activation(out=warm[:, 8:9], in_=warm[:, 0:1], func=ACT.Silu)
+        load_x(0, 0)
+        load_x(0, 1)
+        load_scales(nc.sync, w4_scales, 0, range(QUADS))
+        load_scales(nc.sync, w8_scales, W8_ROW, range(QUADS))
+        load_w4(0, 0, 1)
+        load_w8(0, 0)
+        load_w4(0, 1, GROUPS)
+        load_w8(0, 1)
+        nc.sync.dma_start(out=bias[:], in_=b.rearrange("(g p r) -> p g r", g=GROUPS, r=PACK))
+        load_x(1, 0)
+        load_x(1, 1)
+        load_w4(1, 0, GROUPS)
+        load_w8(1, 0)
+        load_w8(1, 1)
+        load_w8(0, 2)
+        load_w8(1, 2)
+
+        feat_vector("a", 0, 0)
+        feat_scalar("b", 0, 0)
+        feat_vector("a", 0, 1)
+        feat_scalar("b", 0, 1)
+        quant_x("a", 0, 0)
+        quant_x("a", 0, 1)
+        quant_x("b", 0, 0)
+        deal_scales(0, 0)
+        deal_w4(0, 0)
+        for r in range(PACK):
+            mm4(0, 0, r)
+        quant_x("b", 0, 1)
+        deal_w8(0, 0)
+        for r in range(PACK):
+            mm8(0, 0, r)
+        deal_scales(0, 1)
+        deal_w4(0, 1)
+        for r in range(PACK):
+            mm4(0, 1, r)
+        deal_w8(0, 1)
+        for r in range(PACK):
+            mm8(0, 1, r)
+
+        feat_scalar("a", 1, 0)
+        feat_scalar("b", 1, 0)
+        feat_scalar("b", 1, 1)
+        deal_scales(1, 0)
+        quant_x("a", 1, 0)
+        feat_vector("a", 1, 1)
+        deal_w4(1, 0)
+        quant_x("a", 1, 1)
+        quant_x("b", 1, 0)
+        deal_w8(1, 0)
+        quant_x("b", 1, 1)
+        for r in range(PACK):
+            mm4(1, 0, r)
+            mm8(1, 0, r)
+            silu_store(0, r)
+        deal_scales(1, 1)
+        deal_w4(1, 1)
+        deal_w8(1, 1)
+        for r in range(PACK):
+            mm4(1, 1, r)
+            mm8(1, 1, r)
+            silu_store(1, r)
+        for a in range(PASSES):
+            deal_scales(a, 2)
+            deal_w4(a, 2)
+            deal_w8(a, 2)
+        planes(0)
+        for r in range(PACK - 1):
+            for a in range(PASSES):
+                mm4(a, 2, r)
+                mm8(a, 2, r)
+            silu_store(2, r)
+            if r == 0:
+                planes(1)
+        chunks = range(0, T, P)
+        for c0 in chunks:
+            for a in range(PASSES):
+                mm4(a, 2, 3, c0, P)
+                mm8(a, 2, 3, c0, P)
+            silu(2, 3, c0, P)
+            round_y(2, c0, P)
+            if c0 > 0:
+                quant_y(2, c0 - P, P)
+            if c0 == 2 * P:
+                store_codes(2, 0, HALF)
+        store_y(nc.scalar, 2, 3)
+        quant_y(2, T - P, P)
+        store_codes(2, HALF, HALF)
+        for q in range(QUADS):
+            queue = nc.sync if q < 2 else nc.scalar
+            queue.dma_start(
+                out=out_2[:, 4 * q : 4 * q + 4, :].rearrange("g q t -> q g t").bitcast(I32),
+                in_=y_scales[32 * q : 32 * q + 4, :, :].bitcast(I32),
+            )

@@ -37,12 +37,12 @@ def tile_mix_feat_fm_crelupl_silu_kernel(
         def tile(name, shape, dtype):
             return sb.tile(shape, dtype, name=name, align_bytes=64)
 
-        x_raw = {(a, h): tile("x_raw%d%d" % (a, h), [P, PACK, HALF], F32) for a in range(PASSES) for h in range(2)}
+        x_raw = {a: tile("x_raw%d" % a, [P, PACK, T], F32) for a in range(PASSES)}
         feat = {(s, a): tile("feat%s%d" % (s, a), [P, T, PACK], BF16) for s in "ab" for a in range(PASSES)}
         x_codes = {(s, a): tile("x_codes%s%d" % (s, a), [P, T], U32) for s in "ab" for a in range(PASSES)}
         x_scales = {(s, a): tile("x_scales%s%d" % (s, a), [P, T], U8) for s in "ab" for a in range(PASSES)}
         w4_raw = {a: tile("w4_raw%d" % a, [P, 2 * M], U8) for a in range(PASSES)}
-        w8_raw = {(a, g): tile("w8_raw%d%d" % (a, g), [P, SPAN], I32) for a in range(PASSES) for g in range(GROUPS)}
+        w8_raw = {a: tile("w8_raw%d" % a, [P, M], I32) for a in range(PASSES)}
         ws_raw = tile("ws_raw", [P, PASSES, M], U8)
         w4 = {(a, g): tile("w4_%d%d" % (a, g), [P, PACK, 2 * P], U8) for a in range(PASSES) for g in range(GROUPS)}
         w8 = {(a, g): tile("w8_%d%d" % (a, g), [P, PACK, P], I32) for a in range(PASSES) for g in range(GROUPS)}
@@ -55,42 +55,53 @@ def tile_mix_feat_fm_crelupl_silu_kernel(
         warm = tile("warm", [P, 16], F32)
         acc = {}
 
-        def load_x(a, h):
+        def clear_scales():
+            nc.vector.memset(ws_raw[:].rearrange("p a n -> p (a n)").bitcast(I32), 0)
+
+        def warm_up():
+            nc.vector.memset(warm[:], 0.0)
+            nc.scalar.activation(out=warm[:, 8:9], in_=warm[:, 0:1], func=ACT.Silu)
+
+        def load_bias(queue):
+            queue.dma_start(out=bias[:], in_=b.rearrange("(g p r) -> p g r", g=GROUPS, r=PACK))
+
+        def load_x(a, c0, n, queue=nc.sync):
             rows = x[a * SPAN : (a + 1) * SPAN, :].rearrange("(p j) t -> p j t", j=PACK)
-            nc.sync.dma_start(out=x_raw[a, h][:], in_=rows[:, :, h * HALF : (h + 1) * HALF])
+            queue.dma_start(out=x_raw[a][:, :, c0 : c0 + n], in_=rows[:, :, c0 : c0 + n])
 
         def load_w4(a, g0, g1):
             cols = slice(2 * SPAN * g0, 2 * SPAN * g1)
             nc.sync.dma_start(out=w4_raw[a][:, cols].bitcast(I32), in_=w4_words[a][:, cols].bitcast(I32))
 
-        def load_w8(a, g):
-            src = w8_words[a].rearrange("p n i -> p (n i)")
-            nc.sync.dma_start(out=w8_raw[a, g][:], in_=src[:, PACK * SPAN * g : PACK * SPAN * (g + 1)].bitcast(I32))
+        def load_w8(a, g0, g1):
+            cols = slice(SPAN * g0, SPAN * g1)
+            words = w8_words[a].rearrange("p n i -> p (n i)").bitcast(I32)
+            nc.sync.dma_start(out=w8_raw[a][:, cols], in_=words[:, cols])
 
-        def load_scales(queue, src, row, quads):
-            for q in quads:
+        def load_scales(queue, src, row, rows):
+            for u in rows:
                 queue.dma_start(
-                    out=ws_raw[32 * q + row : 32 * q + row + 4, :, :].bitcast(I32),
-                    in_=src[:, 4 * q : 4 * q + 4, :].rearrange("a q n -> q a n").bitcast(I32),
+                    out=ws_raw[row + u : P : 32, :, :].bitcast(I32),
+                    in_=src[:, u : 16 : 4, :].rearrange("a q n -> q a n").bitcast(I32),
                 )
 
-        def feat_views(s, a, h):
-            dst = feat[s, a][:, h * HALF : (h + 1) * HALF, :].rearrange("p (c i) j -> p c j i", i=4)
-            src = x_raw[a, h][:].rearrange("p j (c i) -> p c j i", i=4)
+        def feat_views(s, a, c0, n):
+            dst = feat[s, a][:, c0 : c0 + n, :].rearrange("p (c i) j -> p c j i", i=4)
+            src = x_raw[a][:, :, c0 : c0 + n].rearrange("p j (c i) -> p c j i", i=4)
             return dst, src
 
-        def feat_vector(s, a, h):
-            dst, src = feat_views(s, a, h)
+        def feat_vector(s, a, c0, n):
+            dst, src = feat_views(s, a, c0, n)
             sign = 1.0 if s == "a" else -1.0
             nc.vector.tensor_scalar(out=dst, in0=src, scalar1=sign, scalar2=0.0, op0=ALU.mult, op1=ALU.max)
 
-        def feat_scalar(s, a, h):
-            dst, src = feat_views(s, a, h)
+        def feat_scalar(s, a, c0, n):
+            dst, src = feat_views(s, a, c0, n)
             sign = 1.0 if s == "a" else -1.0
             nc.scalar.activation(out=dst, in_=src, func=ACT.Relu, scale=sign)
 
-        def quant_x(s, a, h):
-            cols = slice(h * HALF, (h + 1) * HALF)
+        def quant_x(s, a, c0, n):
+            cols = slice(c0, c0 + n)
             nc.vector.quantize_mx(
                 out=x_codes[s, a][:, cols].bitcast(FP8X4),
                 scales=x_scales[s, a][:, cols],
@@ -105,40 +116,32 @@ def tile_mix_feat_fm_crelupl_silu_kernel(
             )
 
         def deal_w8(a, g):
+            src = w8_raw[a][:, SPAN * g : SPAN * (g + 1)]
             nc.vector.tensor_copy(
-                out=w8[a, g][:].rearrange("p r m -> p m r"),
-                in_=w8_raw[a, g][:].rearrange("p (m r) -> p m r", r=PACK),
+                out=w8[a, g][:].rearrange("p r m -> p m r"), in_=src.rearrange("p (m r) -> p m r", r=PACK)
             )
 
         def deal_scales(a, g):
             src = ws_raw[:, a, SPAN * g : SPAN * (g + 1)]
             nc.vector.tensor_copy(out=ws[a, g][:], in_=src.rearrange("p (m r) -> p r m", r=PACK))
 
-        def mm4(a, g, r, c0=0, n=T):
-            cols = slice(c0, c0 + n)
-            if a == 0:
-                bank = len(acc) % 8
-                acc[g, r, c0] = ps.tile([P, T], F32, name="acc%d" % len(acc), tag="bank%d" % bank)
-            nc.tensor.matmul_mx(
-                out=acc[g, r, c0][:, 0:n],
-                lhsT=w4[a, g][:, r, :].bitcast(FP4X4),
-                lhsT_scale=ws[a, g][:, r, :],
-                rhs=x_codes["a", a][:, cols].bitcast(FP8X4),
-                rhs_scale=x_scales["a", a][:, cols],
-                start=(a == 0),
-                stop=False,
-            )
+        def open_acc(g, r, c0=0):
+            acc[g, r, c0] = ps.tile([P, T], F32, name="acc%d" % len(acc), tag="bank%d" % (len(acc) % 8))
 
-        def mm8(a, g, r, c0=0, n=T):
+        def mm(w, a, g, r, c0=0, n=T, start=False, stop=False, base=0):
             cols = slice(c0, c0 + n)
+            if w == 4:
+                s, codes, scales = "a", w4[a, g][:, r, :].bitcast(FP4X4), ws[a, g][:, r, :]
+            else:
+                s, codes, scales = "b", w8[a, g][:, r, :].bitcast(FP8X4), ws[a, g][W8_ROW:P, r, :]
             nc.tensor.matmul_mx(
-                out=acc[g, r, c0][:, 0:n],
-                lhsT=w8[a, g][:, r, :].bitcast(FP8X4),
-                lhsT_scale=ws[a, g][W8_ROW:P, r, :],
-                rhs=x_codes["b", a][:, cols].bitcast(FP8X4),
-                rhs_scale=x_scales["b", a][:, cols],
-                start=False,
-                stop=(a == PASSES - 1),
+                out=acc[g, r, base][:, c0 - base : c0 - base + n],
+                lhsT=codes,
+                lhsT_scale=scales,
+                rhs=x_codes[s, a][:, cols].bitcast(FP8X4),
+                rhs_scale=x_scales[s, a][:, cols],
+                start=start,
+                stop=stop,
             )
 
         def silu(g, r, c0=0, n=T):
@@ -146,20 +149,23 @@ def tile_mix_feat_fm_crelupl_silu_kernel(
                 out=y[g][:, r, c0 : c0 + n], in_=acc[g, r, c0][:, 0:n], func=ACT.Silu, bias=bias[:, g, r : r + 1]
             )
 
-        def store_y(queue, g, r):
+        def store_y(queue, g, r0, r1=None, c0=0, n=T):
+            r1 = r1 or r0 + 1
             rows = out_0[g * SPAN : (g + 1) * SPAN, :].rearrange("(p r) t -> p r t", r=PACK)
-            queue.dma_start(out=rows[:, r, :], in_=y[g][:, r, :])
+            queue.dma_start(out=rows[:, r0:r1, c0 : c0 + n], in_=y[g][:, r0:r1, c0 : c0 + n])
 
-        def silu_store(g, r):
-            silu(g, r)
-            store_y(nc.sync, g, r)
+        def round_views(g, c0, n):
+            dst = y_bf[g][:, c0 : c0 + n, :].rearrange("p (c i) r -> p c r i", i=4)
+            src = y[g][:, :, c0 : c0 + n].rearrange("p r (c i) -> p c r i", i=4)
+            return dst, src
 
         def round_y(g, c0, n):
-            cols = slice(c0, c0 + n)
-            nc.vector.tensor_copy(
-                out=y_bf[g][:, cols, :].rearrange("p (c i) r -> p c r i", i=4),
-                in_=y[g][:, :, cols].rearrange("p r (c i) -> p c r i", i=4),
-            )
+            dst, src = round_views(g, c0, n)
+            nc.vector.tensor_copy(out=dst, in_=src)
+
+        def round_y_scalar(g, c0, n):
+            dst, src = round_views(g, c0, n)
+            nc.scalar.copy(out=dst, in_=src)
 
         def quant_y(g, c0, n):
             cols = slice(c0, c0 + n)
@@ -169,113 +175,132 @@ def tile_mix_feat_fm_crelupl_silu_kernel(
                 in_=y_bf[g][:, cols, :].rearrange("p t r -> p (t r)"),
             )
 
-        def store_codes(g, c0, n):
+        def store_codes(queue, g, c0, n):
             cols = slice(c0, c0 + n)
-            nc.sync.dma_start(
-                out=out_1[g].rearrange("p t i -> p (t i)").bitcast(I32)[:, cols], in_=y_codes[g][:, cols].bitcast(I32)
-            )
+            words = out_1[g].rearrange("p t i -> p (t i)").bitcast(I32)
+            queue.dma_start(out=words[:, cols], in_=y_codes[g][:, cols].bitcast(I32))
+
+        def store_scales(queue, rows, g0=0, g1=GROUPS):
+            for u in rows:
+                queue.dma_start(
+                    out=out_2[g0:g1, u : 16 : 4, :].rearrange("g q t -> q g t").bitcast(I32),
+                    in_=y_scales[u : P : 32, g0:g1, :].bitcast(I32),
+                )
 
         def planes(g):
             round_y(g, 0, HALF)
             round_y(g, HALF, HALF)
             quant_y(g, 0, HALF)
             quant_y(g, HALF, HALF)
-            store_codes(g, 0, T)
+            store_codes(nc.sync, g, 0, T)
 
-        nc.vector.memset(ws_raw[:].rearrange("p a n -> p (a n)").bitcast(I32), 0)
-        nc.vector.memset(warm[:], 0.0)
-        nc.scalar.activation(out=warm[:, 8:9], in_=warm[:, 0:1], func=ACT.Silu)
-        load_x(0, 0)
-        load_x(0, 1)
-        load_scales(nc.sync, w4_scales, 0, range(QUADS))
-        load_scales(nc.sync, w8_scales, W8_ROW, range(QUADS))
-        load_w4(0, 0, 1)
-        load_w8(0, 0)
-        load_w4(0, 1, GROUPS)
-        load_w8(0, 1)
-        nc.sync.dma_start(out=bias[:], in_=b.rearrange("(g p r) -> p g r", g=GROUPS, r=PACK))
-        load_x(1, 0)
-        load_x(1, 1)
-        load_w4(1, 0, GROUPS)
-        load_w8(1, 0)
-        load_w8(1, 1)
-        load_w8(0, 2)
-        load_w8(1, 2)
+        clear_scales()
+        warm_up()
+        load_x(0, 0, HALF)
+        load_w8(0, 0, 1)
+        load_scales(nc.sync, w8_scales, W8_ROW, [0])
+        load_scales(nc.sync, w4_scales, 0, [0])
+        load_scales(nc.sync, w8_scales, W8_ROW, [1])
+        load_scales(nc.sync, w4_scales, 0, [1])
+        load_scales(nc.sync, w8_scales, W8_ROW, [2])
+        load_scales(nc.sync, w4_scales, 0, [2])
+        load_scales(nc.sync, w8_scales, W8_ROW, [3])
+        load_scales(nc.sync, w4_scales, 0, [3])
+        load_x(0, HALF, HALF)
+        load_w4(0, 0, 2)
+        load_x(1, 0, HALF)
+        load_w8(0, 1, 2)
+        load_x(1, HALF, HALF)
+        load_w8(1, 0, 1)
+        load_w4(1, 0, 2)
+        load_bias(nc.sync)
+        load_w8(1, 1, 3)
+        load_w8(0, 2, 3)
+        load_w4(0, 2, 3)
+        load_w4(1, 2, 3)
 
-        feat_vector("a", 0, 0)
-        feat_scalar("b", 0, 0)
-        feat_vector("a", 0, 1)
-        feat_scalar("b", 0, 1)
-        quant_x("a", 0, 0)
-        quant_x("a", 0, 1)
-        quant_x("b", 0, 0)
-        deal_scales(0, 0)
-        deal_w4(0, 0)
-        for r in range(PACK):
-            mm4(0, 0, r)
-        quant_x("b", 0, 1)
+        feat_vector("b", 0, 0, HALF)
+        feat_scalar("a", 0, 0, HALF)
         deal_w8(0, 0)
+        quant_x("b", 0, 0, HALF)
+        quant_x("a", 0, 0, HALF)
+        deal_scales(0, 0)
         for r in range(PACK):
-            mm8(0, 0, r)
+            open_acc(0, r)
+            mm(8, 0, 0, r, 0, HALF, start=True)
         deal_scales(0, 1)
+        deal_scales(1, 0)
+        feat_vector("b", 0, HALF, HALF)
+        feat_scalar("a", 0, HALF, HALF)
+        deal_scales(1, 1)
+        quant_x("b", 0, HALF, HALF)
+        for r in range(PACK):
+            mm(8, 0, 0, r, HALF, HALF)
+        deal_w4(0, 0)
+        quant_x("a", 0, HALF, HALF)
+        for r in range(PACK):
+            mm(4, 0, 0, r)
         deal_w4(0, 1)
         for r in range(PACK):
-            mm4(0, 1, r)
+            open_acc(1, r)
+            mm(4, 0, 1, r, start=True)
         deal_w8(0, 1)
         for r in range(PACK):
-            mm8(0, 1, r)
-
-        feat_scalar("a", 1, 0)
-        feat_scalar("b", 1, 0)
-        feat_scalar("b", 1, 1)
-        deal_scales(1, 0)
-        quant_x("a", 1, 0)
-        feat_vector("a", 1, 1)
-        deal_w4(1, 0)
-        quant_x("a", 1, 1)
-        quant_x("b", 1, 0)
+            mm(8, 0, 1, r)
+        feat_scalar("b", 1, 0, HALF)
+        feat_scalar("a", 1, 0, HALF)
+        feat_scalar("a", 1, HALF, HALF)
+        quant_x("b", 1, 0, HALF)
+        feat_vector("b", 1, HALF, HALF)
         deal_w8(1, 0)
-        quant_x("b", 1, 1)
-        for r in range(PACK):
-            mm4(1, 0, r)
-            mm8(1, 0, r)
-            silu_store(0, r)
-        deal_scales(1, 1)
-        deal_w4(1, 1)
-        deal_w8(1, 1)
-        for r in range(PACK):
-            mm4(1, 1, r)
-            mm8(1, 1, r)
-            silu_store(1, r)
+        quant_x("b", 1, HALF, HALF)
+        quant_x("a", 1, 0, HALF)
+        deal_w4(1, 0)
+        quant_x("a", 1, HALF, HALF)
+
+        for g in range(2):
+            for r in range(PACK):
+                mm(8, 1, g, r)
+                mm(4, 1, g, r, stop=True)
+                silu(g, r)
+                if g == 0 and r < 2:
+                    store_y(nc.sync, g, r)
+                elif r % 2 == 1:
+                    store_y(nc.sync, g, r - 1, r + 1)
+            if g == 0:
+                deal_w8(1, 1)
+                deal_w4(1, 1)
         for a in range(PASSES):
             deal_scales(a, 2)
-            deal_w4(a, 2)
             deal_w8(a, 2)
+            deal_w4(a, 2)
         planes(0)
+
         for r in range(PACK - 1):
+            open_acc(2, r)
             for a in range(PASSES):
-                mm4(a, 2, r)
-                mm8(a, 2, r)
-            silu_store(2, r)
+                mm(8, a, 2, r, start=(a == 0))
+                mm(4, a, 2, r, stop=(a == 1))
+            silu(2, r)
+            store_y(nc.sync, 2, r)
             if r == 0:
                 planes(1)
-        chunks = range(0, T, P)
-        for c0 in chunks:
+            if r == 1:
+                store_scales(nc.sync, range(4), 0, 2)
+        for c0 in range(0, T, P):
+            open_acc(2, 3, c0)
             for a in range(PASSES):
-                mm4(a, 2, 3, c0, P)
-                mm8(a, 2, 3, c0, P)
+                mm(8, a, 2, 3, c0, P, start=(a == 0), base=c0)
+                mm(4, a, 2, 3, c0, P, stop=(a == 1), base=c0)
             silu(2, 3, c0, P)
+        store_y(nc.scalar, 2, 3)
+        for c0 in range(0, T, P):
             round_y(2, c0, P)
             if c0 > 0:
                 quant_y(2, c0 - P, P)
             if c0 == 2 * P:
-                store_codes(2, 0, HALF)
-        store_y(nc.scalar, 2, 3)
+                store_codes(nc.sync, 2, 0, HALF)
         quant_y(2, T - P, P)
-        store_codes(2, HALF, HALF)
-        for q in range(QUADS):
-            queue = nc.sync if q < 2 else nc.scalar
-            queue.dma_start(
-                out=out_2[:, 4 * q : 4 * q + 4, :].rearrange("g q t -> q g t").bitcast(I32),
-                in_=y_scales[32 * q : 32 * q + 4, :, :].bitcast(I32),
-            )
+        store_codes(nc.sync, 2, HALF, HALF)
+        store_scales(nc.sync, [0, 1], 2, 3)
+        store_scales(nc.scalar, [2, 3], 2, 3)

@@ -187,43 +187,33 @@ def tile_mix_feat_fm_crelupl_silu_kernel(
                     in_=y_scales[u : P : 32, g0:g1, :].bitcast(I32),
                 )
 
-        def planes(g):
-            round_y(g, 0, HALF)
-            round_y(g, HALF, HALF)
-            quant_y(g, 0, HALF)
-            quant_y(g, HALF, HALF)
-            store_codes(nc.sync, g, 0, T)
-
         clear_scales()
         warm_up()
-        load_x(0, 0, HALF)
-        load_w8(0, 0, 1)
-        load_scales(nc.sync, w8_scales, W8_ROW, [0])
-        load_scales(nc.sync, w4_scales, 0, [0])
-        load_scales(nc.sync, w8_scales, W8_ROW, [1])
-        load_scales(nc.sync, w4_scales, 0, [1])
-        load_scales(nc.sync, w8_scales, W8_ROW, [2])
-        load_scales(nc.sync, w4_scales, 0, [2])
-        load_scales(nc.sync, w8_scales, W8_ROW, [3])
-        load_scales(nc.sync, w4_scales, 0, [3])
-        load_x(0, HALF, HALF)
         load_w4(0, 0, 2)
+        load_x(0, 0, HALF)
+        for u in range(4):
+            load_scales(nc.sync, w8_scales, W8_ROW, [u])
+            load_scales(nc.sync, w4_scales, 0, [u])
+            if u == 0:
+                load_w8(0, 0, 1)
+        load_x(0, HALF, HALF)
         load_x(1, 0, HALF)
         load_w8(0, 1, 2)
         load_x(1, HALF, HALF)
-        load_w8(1, 0, 1)
         load_w4(1, 0, 2)
+        load_w8(1, 0, 1)
         load_bias(nc.sync)
-        load_w8(1, 1, 3)
+        load_w8(1, 1, 2)
         load_w8(0, 2, 3)
         load_w4(0, 2, 3)
         load_w4(1, 2, 3)
-
-        feat_vector("b", 0, 0, HALF)
+        load_w8(1, 2, 3)
+        deal_w4(0, 0)
+        deal_w4(0, 1)
+        feat_scalar("b", 0, 0, HALF)
         feat_scalar("a", 0, 0, HALF)
         deal_w8(0, 0)
         quant_x("b", 0, 0, HALF)
-        quant_x("a", 0, 0, HALF)
         deal_scales(0, 0)
         for r in range(PACK):
             open_acc(0, r)
@@ -232,18 +222,17 @@ def tile_mix_feat_fm_crelupl_silu_kernel(
         deal_scales(1, 0)
         feat_vector("b", 0, HALF, HALF)
         feat_scalar("a", 0, HALF, HALF)
-        deal_scales(1, 1)
+        quant_x("a", 0, 0, HALF)
         quant_x("b", 0, HALF, HALF)
         for r in range(PACK):
             mm(8, 0, 0, r, HALF, HALF)
-        deal_w4(0, 0)
+        deal_scales(1, 1)
         quant_x("a", 0, HALF, HALF)
-        for r in range(PACK):
-            mm(4, 0, 0, r)
-        deal_w4(0, 1)
-        for r in range(PACK):
-            open_acc(1, r)
-            mm(4, 0, 1, r, start=True)
+        for g in range(2):
+            for r in range(PACK):
+                if g == 1:
+                    open_acc(1, r)
+                mm(4, 0, g, r, start=(g == 1))
         deal_w8(0, 1)
         for r in range(PACK):
             mm(8, 0, 1, r)
@@ -252,12 +241,11 @@ def tile_mix_feat_fm_crelupl_silu_kernel(
         feat_scalar("a", 1, HALF, HALF)
         quant_x("b", 1, 0, HALF)
         feat_vector("b", 1, HALF, HALF)
-        deal_w8(1, 0)
-        quant_x("b", 1, HALF, HALF)
-        quant_x("a", 1, 0, HALF)
         deal_w4(1, 0)
+        quant_x("b", 1, HALF, HALF)
+        deal_w8(1, 0)
+        quant_x("a", 1, 0, HALF)
         quant_x("a", 1, HALF, HALF)
-
         for g in range(2):
             for r in range(PACK):
                 mm(8, 1, g, r)
@@ -268,13 +256,21 @@ def tile_mix_feat_fm_crelupl_silu_kernel(
                 elif r % 2 == 1:
                     store_y(nc.sync, g, r - 1, r + 1)
             if g == 0:
-                deal_w8(1, 1)
                 deal_w4(1, 1)
+                deal_w8(1, 1)
         for a in range(PASSES):
             deal_scales(a, 2)
             deal_w8(a, 2)
             deal_w4(a, 2)
-        planes(0)
+        round_y(0, 0, HALF)
+        round_y(0, HALF, HALF)
+        quant_y(0, 0, HALF)
+        quant_y(0, HALF, HALF)
+        store_codes(nc.sync, 0, 0, T)
+        round_y(1, 0, HALF)
+        round_y_scalar(1, HALF, HALF)
+        quant_y(1, 0, HALF)
+        quant_y(1, HALF, HALF)
 
         for r in range(PACK - 1):
             open_acc(2, r)
@@ -284,23 +280,22 @@ def tile_mix_feat_fm_crelupl_silu_kernel(
             silu(2, r)
             store_y(nc.sync, 2, r)
             if r == 0:
-                planes(1)
-            if r == 1:
-                store_scales(nc.sync, range(4), 0, 2)
+                store_codes(nc.sync, 1, 0, T)
         for c0 in range(0, T, P):
             open_acc(2, 3, c0)
             for a in range(PASSES):
                 mm(8, a, 2, 3, c0, P, start=(a == 0), base=c0)
                 mm(4, a, 2, 3, c0, P, stop=(a == 1), base=c0)
             silu(2, 3, c0, P)
-        store_y(nc.scalar, 2, 3)
+        store_y(nc.sync, 2, 3)
         for c0 in range(0, T, P):
-            round_y(2, c0, P)
+            if c0 == 3 * P:
+                round_y_scalar(2, c0, P)
+            else:
+                round_y(2, c0, P)
             if c0 > 0:
                 quant_y(2, c0 - P, P)
-            if c0 == 2 * P:
-                store_codes(nc.sync, 2, 0, HALF)
         quant_y(2, T - P, P)
-        store_codes(nc.sync, 2, HALF, HALF)
-        store_scales(nc.sync, [0, 1], 2, 3)
-        store_scales(nc.scalar, [2, 3], 2, 3)
+        store_codes(nc.sync, 2, 0, T)
+        store_scales(nc.scalar, [0, 1])
+        store_scales(nc.sync, [2, 3])

@@ -190,61 +190,62 @@ def tile_mix_feat_fm_crelupl_silu_kernel(
         clear_scales()
         warm_up()
         load_w4(0, 0, 2)
-        load_x(0, 0, HALF)
         for u in range(4):
-            load_scales(nc.sync, w8_scales, W8_ROW, [u])
             load_scales(nc.sync, w4_scales, 0, [u])
+            load_scales(nc.sync, w8_scales, W8_ROW, [u])
             if u == 0:
-                load_w8(0, 0, 1)
+                load_x(0, 0, HALF)
         load_x(0, HALF, HALF)
         load_x(1, 0, HALF)
-        load_w8(0, 1, 2)
+        load_w8(0, 0, 1)
         load_x(1, HALF, HALF)
-        load_w4(1, 0, 2)
+        load_w8(0, 1, 2)
         load_w8(1, 0, 1)
+        load_w4(1, 0, 2)
         load_bias(nc.sync)
         load_w8(1, 1, 2)
-        load_w8(0, 2, 3)
         load_w4(0, 2, 3)
+        load_w8(0, 2, 3)
         load_w4(1, 2, 3)
         load_w8(1, 2, 3)
         deal_w4(0, 0)
         deal_w4(0, 1)
+        feat_vector("a", 0, 0, HALF)
         feat_scalar("b", 0, 0, HALF)
-        feat_scalar("a", 0, 0, HALF)
-        deal_w8(0, 0)
-        quant_x("b", 0, 0, HALF)
-        deal_scales(0, 0)
-        for r in range(PACK):
-            open_acc(0, r)
-            mm(8, 0, 0, r, 0, HALF, start=True)
-        deal_scales(0, 1)
-        deal_scales(1, 0)
-        feat_vector("b", 0, HALF, HALF)
-        feat_scalar("a", 0, HALF, HALF)
         quant_x("a", 0, 0, HALF)
-        quant_x("b", 0, HALF, HALF)
-        for r in range(PACK):
-            mm(8, 0, 0, r, HALF, HALF)
-        deal_scales(1, 1)
-        quant_x("a", 0, HALF, HALF)
+        deal_scales(0, 0)
+        deal_scales(0, 1)
         for g in range(2):
             for r in range(PACK):
-                if g == 1:
-                    open_acc(1, r)
-                mm(4, 0, g, r, start=(g == 1))
+                open_acc(g, r)
+                for c0 in (0, P):
+                    mm(4, 0, g, r, c0, P, start=(c0 == 0))
+        feat_vector("a", 0, HALF, HALF)
+        feat_scalar("b", 0, HALF, HALF)
+        quant_x("b", 0, 0, HALF)
+        quant_x("a", 0, HALF, HALF)
+        deal_scales(1, 0)
+        deal_scales(1, 1)
+        for g in range(2):
+            for r in range(PACK):
+                for c0 in (2 * P, 3 * P):
+                    mm(4, 0, g, r, c0, P)
+        feat_scalar("b", 1, 0, HALF)
+        feat_scalar("a", 1, 0, HALF)
+        feat_scalar("b", 1, HALF, HALF)
+        deal_w8(0, 0)
+        quant_x("b", 0, HALF, HALF)
+        for r in range(PACK):
+            mm(8, 0, 0, r)
+        quant_x("b", 1, 0, HALF)
+        feat_vector("a", 1, HALF, HALF)
         deal_w8(0, 1)
         for r in range(PACK):
             mm(8, 0, 1, r)
-        feat_scalar("b", 1, 0, HALF)
-        feat_scalar("a", 1, 0, HALF)
-        feat_scalar("a", 1, HALF, HALF)
-        quant_x("b", 1, 0, HALF)
-        feat_vector("b", 1, HALF, HALF)
+        quant_x("a", 1, 0, HALF)
+        deal_w8(1, 0)
         deal_w4(1, 0)
         quant_x("b", 1, HALF, HALF)
-        deal_w8(1, 0)
-        quant_x("a", 1, 0, HALF)
         quant_x("a", 1, HALF, HALF)
         for g in range(2):
             for r in range(PACK):
@@ -268,7 +269,7 @@ def tile_mix_feat_fm_crelupl_silu_kernel(
         quant_y(0, HALF, HALF)
         store_codes(nc.sync, 0, 0, T)
         round_y(1, 0, HALF)
-        round_y_scalar(1, HALF, HALF)
+        round_y(1, HALF, HALF)
         quant_y(1, 0, HALF)
         quant_y(1, HALF, HALF)
 

from contextlib import ExitStack

import concourse.mybir as mybir

K, M, T = 1024, 1536, 512
FLOPS = 2 * 2 * K * M * T

F32 = mybir.dt.float32
BF16 = mybir.dt.bfloat16
I32 = mybir.dt.int32
U32 = mybir.dt.uint32
U8 = mybir.dt.uint8
FP8X4 = mybir.dt.float8_e4m3fn_x4
FP4X4 = mybir.dt.float4_e2m1fn_x4
ALU = mybir.AluOpType
ACT = mybir.ActivationFunctionType

P = 128
PACK = 4
SPAN = P * PACK
PASSES = K // SPAN
GROUPS = M // SPAN
HALF = T // 2
QUADS = 4
W8_ROW = 4


def tile_mix_feat_fm_crelupl_silu_kernel(
    tc, x, w4_words, w4_scales, w8_words, w8_scales, b, out_0, out_1, out_2
):
    nc = tc.nc
    with ExitStack() as ctx:
        sb = ctx.enter_context(tc.tile_pool(name="sb", bufs=1))
        ps = ctx.enter_context(tc.psum_pool(name="ps", bufs=1))
        ctx.enter_context(tc.manual_schedule())

        def tile(name, shape, dtype):
            return sb.tile(shape, dtype, name=name, align_bytes=64)

        x_raw = {a: tile("x_raw%d" % a, [P, PACK, T], F32) for a in range(PASSES)}
        feat = {(s, a): tile("feat%s%d" % (s, a), [P, T, PACK], BF16) for s in "ab" for a in range(PASSES)}
        x_codes = {(s, a): tile("x_codes%s%d" % (s, a), [P, T], U32) for s in "ab" for a in range(PASSES)}
        x_scales = {(s, a): tile("x_scales%s%d" % (s, a), [P, T], U8) for s in "ab" for a in range(PASSES)}
        w4_raw = {a: tile("w4_raw%d" % a, [P, 2 * M], U8) for a in range(PASSES)}
        w8_raw = {a: tile("w8_raw%d" % a, [P, M], I32) for a in range(PASSES)}
        ws_raw = tile("ws_raw", [P, PASSES, M], U8)
        w4 = {(a, g): tile("w4_%d%d" % (a, g), [P, PACK, 2 * P], U8) for a in range(PASSES) for g in range(GROUPS)}
        w8 = {(a, g): tile("w8_%d%d" % (a, g), [P, PACK, P], I32) for a in range(PASSES) for g in range(GROUPS)}
        ws = {(a, g): tile("ws_%d%d" % (a, g), [P, PACK, P], U8) for a in range(PASSES) for g in range(GROUPS)}
        bias = tile("bias", [P, GROUPS, PACK], F32)
        y = {g: tile("y%d" % g, [P, PACK, T], F32) for g in range(GROUPS)}
        y_bf = {g: tile("y_bf%d" % g, [P, T, PACK], BF16) for g in range(GROUPS)}
        y_codes = {g: tile("y_codes%d" % g, [P, T], U32) for g in range(GROUPS)}
        y_scales = tile("y_scales", [P, GROUPS, T], U8)
        warm = tile("warm", [P, 16], F32)
        acc = {}

        def clear_scales():
            nc.vector.memset(ws_raw[:].rearrange("p a n -> p (a n)").bitcast(I32), 0)

        def warm_up():
            nc.vector.memset(warm[:], 0.0)
            nc.scalar.activation(out=warm[:, 8:9], in_=warm[:, 0:1], func=ACT.Silu)

        def load_bias(queue):
            queue.dma_start(out=bias[:], in_=b.rearrange("(g p r) -> p g r", g=GROUPS, r=PACK))

        def load_x(a, c0, n, queue=nc.sync):
            rows = x[a * SPAN : (a + 1) * SPAN, :].rearrange("(p j) t -> p j t", j=PACK)
            queue.dma_start(out=x_raw[a][:, :, c0 : c0 + n], in_=rows[:, :, c0 : c0 + n])

        def load_w4(a, g0, g1):
            cols = slice(2 * SPAN * g0, 2 * SPAN * g1)
            nc.sync.dma_start(out=w4_raw[a][:, cols].bitcast(I32), in_=w4_words[a][:, cols].bitcast(I32))

        def load_w8(a, g0, g1):
            cols = slice(SPAN * g0, SPAN * g1)
            words = w8_words[a].rearrange("p n i -> p (n i)").bitcast(I32)
            nc.sync.dma_start(out=w8_raw[a][:, cols], in_=words[:, cols])

        def load_scales(queue, src, row, rows):
            for u in rows:
                queue.dma_start(
                    out=ws_raw[row + u : P : 32, :, :].bitcast(I32),
                    in_=src[:, u : 16 : 4, :].rearrange("a q n -> q a n").bitcast(I32),
                )

        def feat_views(s, a, c0, n):
            dst = feat[s, a][:, c0 : c0 + n, :].rearrange("p (c i) j -> p c j i", i=4)
            src = x_raw[a][:, :, c0 : c0 + n].rearrange("p j (c i) -> p c j i", i=4)
            return dst, src

        def feat_vector(s, a, c0, n):
            dst, src = feat_views(s, a, c0, n)
            sign = 1.0 if s == "a" else -1.0
            nc.vector.tensor_scalar(out=dst, in0=src, scalar1=sign, scalar2=0.0, op0=ALU.mult, op1=ALU.max)

        def feat_scalar(s, a, c0, n):
            dst, src = feat_views(s, a, c0, n)
            sign = 1.0 if s == "a" else -1.0
            nc.scalar.activation(out=dst, in_=src, func=ACT.Relu, scale=sign)

        def quant_x(s, a, c0, n):
            cols = slice(c0, c0 + n)
            nc.vector.quantize_mx(
                out=x_codes[s, a][:, cols].bitcast(FP8X4),
                scales=x_scales[s, a][:, cols],
                in_=feat[s, a][:, cols, :].rearrange("p t j -> p (t j)"),
            )

        def deal_w4(a, g):
            src = w4_raw[a][:, 2 * SPAN * g : 2 * SPAN * (g + 1)]
            nc.vector.tensor_copy(
                out=w4[a, g][:].rearrange("p r (m e) -> p r m e", e=2),
                in_=src.rearrange("p (m r e) -> p r m e", r=PACK, e=2),
            )

        def deal_w8(a, g):
            src = w8_raw[a][:, SPAN * g : SPAN * (g + 1)]
            nc.vector.tensor_copy(
                out=w8[a, g][:].rearrange("p r m -> p m r"), in_=src.rearrange("p (m r) -> p m r", r=PACK)
            )

        def deal_scales(a, g):
            src = ws_raw[:, a, SPAN * g : SPAN * (g + 1)]
            nc.vector.tensor_copy(out=ws[a, g][:], in_=src.rearrange("p (m r) -> p r m", r=PACK))

        def open_acc(g, r, c0=0):
            acc[g, r, c0] = ps.tile([P, T], F32, name="acc%d" % len(acc), tag="bank%d" % (len(acc) % 8))

        def mm(w, a, g, r, c0=0, n=T, start=False, stop=False, base=0):
            cols = slice(c0, c0 + n)
            if w == 4:
                s, codes, scales = "a", w4[a, g][:, r, :].bitcast(FP4X4), ws[a, g][:, r, :]
            else:
                s, codes, scales = "b", w8[a, g][:, r, :].bitcast(FP8X4), ws[a, g][W8_ROW:P, r, :]
            nc.tensor.matmul_mx(
                out=acc[g, r, base][:, c0 - base : c0 - base + n],
                lhsT=codes,
                lhsT_scale=scales,
                rhs=x_codes[s, a][:, cols].bitcast(FP8X4),
                rhs_scale=x_scales[s, a][:, cols],
                start=start,
                stop=stop,
            )

        def silu(g, r, c0=0, n=T):
            nc.scalar.activation(
                out=y[g][:, r, c0 : c0 + n], in_=acc[g, r, c0][:, 0:n], func=ACT.Silu, bias=bias[:, g, r : r + 1]
            )

        def store_y(queue, g, r0, r1=None, c0=0, n=T):
            r1 = r1 or r0 + 1
            rows = out_0[g * SPAN : (g + 1) * SPAN, :].rearrange("(p r) t -> p r t", r=PACK)
            queue.dma_start(out=rows[:, r0:r1, c0 : c0 + n], in_=y[g][:, r0:r1, c0 : c0 + n])

        def round_views(g, c0, n):
            dst = y_bf[g][:, c0 : c0 + n, :].rearrange("p (c i) r -> p c r i", i=4)
            src = y[g][:, :, c0 : c0 + n].rearrange("p r (c i) -> p c r i", i=4)
            return dst, src

        def round_y(g, c0, n):
            dst, src = round_views(g, c0, n)
            nc.vector.tensor_copy(out=dst, in_=src)

        def round_y_scalar(g, c0, n):
            dst, src = round_views(g, c0, n)
            nc.scalar.copy(out=dst, in_=src)

        def quant_y(g, c0, n):
            cols = slice(c0, c0 + n)
            nc.vector.quantize_mx(
                out=y_codes[g][:, cols].bitcast(FP8X4),
                scales=y_scales[:, g, cols],
                in_=y_bf[g][:, cols, :].rearrange("p t r -> p (t r)"),
            )

        def store_codes(queue, g, c0, n):
            cols = slice(c0, c0 + n)
            words = out_1[g].rearrange("p t i -> p (t i)").bitcast(I32)
            queue.dma_start(out=words[:, cols], in_=y_codes[g][:, cols].bitcast(I32))

        def store_scales(queue, rows, g0=0, g1=GROUPS):
            for u in rows:
                queue.dma_start(
                    out=out_2[g0:g1, u : 16 : 4, :].rearrange("g q t -> q g t").bitcast(I32),
                    in_=y_scales[u : P : 32, g0:g1, :].bitcast(I32),
                )

        clear_scales()
        warm_up()
        load_w4(0, 0, 2)
        for u in range(4):
            load_scales(nc.sync, w4_scales, 0, [u])
            load_scales(nc.sync, w8_scales, W8_ROW, [u])
            if u == 0:
                load_x(0, 0, HALF)
        load_x(0, HALF, HALF)
        load_x(1, 0, HALF)
        load_w8(0, 0, 1)
        load_x(1, HALF, HALF)
        load_w8(0, 1, 2)
        load_w8(1, 0, 1)
        load_w4(1, 0, 2)
        load_bias(nc.sync)
        load_w8(1, 1, 2)
        load_w4(0, 2, 3)
        load_w8(0, 2, 3)
        load_w4(1, 2, 3)
        load_w8(1, 2, 3)
        deal_w4(0, 0)
        deal_w4(0, 1)
        feat_vector("a", 0, 0, HALF)
        feat_scalar("b", 0, 0, HALF)
        quant_x("a", 0, 0, HALF)
        deal_scales(0, 0)
        deal_scales(0, 1)
        for g in range(2):
            for r in range(PACK):
                open_acc(g, r)
                for c0 in (0, P):
                    mm(4, 0, g, r, c0, P, start=(c0 == 0))
        feat_vector("a", 0, HALF, HALF)
        feat_scalar("b", 0, HALF, HALF)
        quant_x("b", 0, 0, HALF)
        quant_x("a", 0, HALF, HALF)
        deal_scales(1, 0)
        deal_scales(1, 1)
        for g in range(2):
            for r in range(PACK):
                for c0 in (2 * P, 3 * P):
                    mm(4, 0, g, r, c0, P)
        feat_scalar("b", 1, 0, HALF)
        feat_scalar("a", 1, 0, HALF)
        feat_scalar("b", 1, HALF, HALF)
        deal_w8(0, 0)
        quant_x("b", 0, HALF, HALF)
        for r in range(PACK):
            mm(8, 0, 0, r)
        quant_x("b", 1, 0, HALF)
        feat_vector("a", 1, HALF, HALF)
        deal_w8(0, 1)
        for r in range(PACK):
            mm(8, 0, 1, r)
        quant_x("a", 1, 0, HALF)
        deal_w8(1, 0)
        deal_w4(1, 0)
        quant_x("b", 1, HALF, HALF)
        quant_x("a", 1, HALF, HALF)
        for g in range(2):
            for r in range(PACK):
                mm(8, 1, g, r)
                mm(4, 1, g, r, stop=True)
                silu(g, r)
                if g == 0 and r < 2:
                    store_y(nc.sync, g, r)
                elif r % 2 == 1:
                    store_y(nc.sync, g, r - 1, r + 1)
            if g == 0:
                deal_w4(1, 1)
                deal_w8(1, 1)
        for a in range(PASSES):
            deal_scales(a, 2)
            deal_w8(a, 2)
            deal_w4(a, 2)
        round_y(0, 0, HALF)
        round_y(0, HALF, HALF)
        quant_y(0, 0, HALF)
        quant_y(0, HALF, HALF)
        store_codes(nc.sync, 0, 0, T)
        round_y(1, 0, HALF)
        round_y(1, HALF, HALF)
        quant_y(1, 0, HALF)
        quant_y(1, HALF, HALF)

        for r in range(PACK - 1):
            open_acc(2, r)
            for a in range(PASSES):
                mm(8, a, 2, r, start=(a == 0))
                mm(4, a, 2, r, stop=(a == 1))
            silu(2, r)
            store_y(nc.sync, 2, r)
            if r == 0:
                store_codes(nc.sync, 1, 0, T)
        for c0 in range(0, T, P):
            open_acc(2, 3, c0)
            for a in range(PASSES):
                mm(8, a, 2, 3, c0, P, start=(a == 0), base=c0)
                mm(4, a, 2, 3, c0, P, stop=(a == 1), base=c0)
            silu(2, 3, c0, P)
        store_y(nc.sync, 2, 3)
        for c0 in range(0, T, P):
            if c0 == 3 * P:
                round_y_scalar(2, c0, P)
            else:
                round_y(2, c0, P)
            if c0 > 0:
                quant_y(2, c0 - P, P)
        quant_y(2, T - P, P)
        store_codes(nc.sync, 2, 0, T)
        store_scales(nc.scalar, [0, 1])
        store_scales(nc.sync, [2, 3])
